import numpy as np
import ml_dtypes


def mxq(x, axis, fmt="e4m3"):
    dtype, down = {"e4m3": (ml_dtypes.float8_e4m3fn, 7), "e5m2": (ml_dtypes.float8_e5m2, 14)}[fmt]
    v = np.moveaxis(np.asarray(x, np.float32).astype(ml_dtypes.bfloat16).astype(np.float64), axis, -1)
    blocks = v.reshape(v.shape[:-1] + (-1, 32))
    amax = np.abs(blocks).max(-1, keepdims=True)
    byte = np.maximum(np.where(amax > 0, np.frexp(amax)[1] - 1 + 127, 0) - down, 1)
    scale = np.exp2(byte - 127.0)
    codes = (blocks / scale).astype(np.float32).astype(dtype).astype(np.float64)
    return np.moveaxis((codes * scale).reshape(v.shape), -1, axis)


WIDE = False


def mx_kscale(k):
    if not WIDE:
        return np.ones(k)
    levels = np.array([10, -10, 5, -5, 0])
    if k % 512:
        return np.exp2(np.random.permutation(np.resize(levels, k // 32))).repeat(32)
    a = np.empty((k // 512, 16))
    for p in range(k // 512):
        a[p, :8] = np.random.permutation(np.resize(levels, 8))
        for g in range(8):
            far = levels[np.abs(levels - a[p, g]) >= 10]
            a[p, g + 8] = far[np.random.randint(len(far))]
    return np.exp2(a.ravel()).repeat(32)


def f64(x):
    return np.asarray(x).astype(np.float64)


def striped(idx):
    return np.tile(idx.reshape(-1, 16).T, (8, 1)).astype(np.uint16)


def unstriped(offs):
    return offs[:16].T.reshape(-1).astype(np.int64)


E2M1 = np.array([0.0, 0.5, 1.0, 1.5, 2.0, 3.0, 4.0, 6.0, -0.0, -0.5, -1.0, -1.5, -2.0, -3.0, -4.0, -6.0])


def pack_weight(w, fmt):
    k, n = w.shape
    w = f64(np.asarray(w, np.float32).astype(ml_dtypes.bfloat16)).reshape(k // 32, 32, n)
    amax = np.abs(w).max(1)
    if fmt == "e4m3":
        byte = np.frexp(amax)[1] - 1 + 127 - 7
    else:
        mant, ex = np.frexp(amax / 6.0)
        byte = np.where(mant > 0.5, ex, ex - 1) + 127
    byte = np.clip(np.where(amax > 0, byte, 1), 1, 254)
    scaled = (w * np.exp2(127.0 - byte)[:, None, :]).reshape(k, n).astype(np.float32)
    by_word = np.ascontiguousarray(scaled.reshape(k // 512, 128, 4, n).transpose(0, 1, 3, 2))
    if fmt == "e4m3":
        words = by_word.astype(ml_dtypes.float8_e4m3fn).view(np.uint8)
    else:
        c = by_word.astype(ml_dtypes.float4_e2m1fn).view(np.uint8) & 0xF
        words = (c[..., 0::2] | (c[..., 1::2] << 4)).reshape(k // 512, 128, 2 * n)
    return np.ascontiguousarray(words), np.ascontiguousarray(byte.astype(np.uint8).reshape(k // 512, 16, n))


def unpack_weight(words, scales, fmt):
    g, _, n = scales.shape
    words = np.ascontiguousarray(words).reshape(g, 128, n, -1)
    if fmt == "e4m3":
        vals = words.view(ml_dtypes.float8_e4m3fn).astype(np.float64)
    else:
        nib = np.empty((g, 128, n, 4), np.uint8)
        nib[..., 0::2] = words & 0xF
        nib[..., 1::2] = words >> 4
        vals = E2M1[nib]
    vals = vals * np.repeat(np.exp2(scales.astype(np.float64) - 127.0), 8, axis=1)[..., None]
    return vals.transpose(0, 1, 3, 2).reshape(g * 512, n)


def gelu(v):
    return 0.5 * v * (1.0 + np.tanh(np.sqrt(2.0 / np.pi) * (v + 0.044715 * v**3)))


K, T, S, P, H, N = 1536, 4096, 1024, 512, 1024, 384


def setup_inputs():
    n = np.random.standard_normal
    s = mx_kscale(K)[:, None]
    u = mx_kscale(H)[:, None]
    d = {}
    d["tab_words"], d["tab_scales"] = pack_weight(n((K, T)) * s, "e2m1")
    d["offs"] = striped(np.random.permutation(T)[:S])
    d["pos1"] = striped(np.random.permutation(S)[:P])
    d["pos2"] = striped(np.random.permutation(S)[:P])
    d["w1"] = (n((K, H)) * 1.2 / K**0.5 / s).astype(np.float32)
    d["moist"] = (0.8 * n((H, P))).astype(np.float32)
    d["gain"] = (np.exp(0.3 * n(H)) * u[:, 0]).astype(np.float32)
    d["w4_words"], d["w4_scales"] = pack_weight(n((H, N)) * 1.3 / H**0.5 / u, "e2m1")
    return d


def reference(tab_words, tab_scales, offs, pos1, pos2, w1, moist, gain, w4_words, w4_scales):
    v = unpack_weight(tab_words, tab_scales, "e2m1")[:, unstriped(offs)]
    w4 = unpack_weight(w4_words, w4_scales, "e2m1")
    mo = f64(moist)
    h = mxq(f64(w1), 0, "e4m3").T @ v
    inner = np.tanh(h[:, unstriped(pos1)] + mo)
    outer = h[:, unstriped(pos2)] - mo
    x = np.concatenate([inner, outer], axis=1) * f64(gain)[:, None]
    y = w4.T @ mxq(x, 0, "e4m3")
    return y[:, :P] / (1.0 + np.abs(y[:, P:]))

@@ -1,0 +1,366 @@
+from contextlib import ExitStack
+
+import concourse.mybir as mybir
+
+K, T, S, M, H, N = 1536, 4096, 1024, 512, 1024, 384
+FLOPS = 2 * K * H * S + 2 * H * N * 2 * M
+
+F32 = mybir.dt.float32
+BF16 = mybir.dt.bfloat16
+I32 = mybir.dt.int32
+U32 = mybir.dt.uint32
+U16 = mybir.dt.uint16
+U8 = mybir.dt.uint8
+FP8X4 = mybir.dt.float8_e4m3fn_x4
+FP4X4 = mybir.dt.float4_e2m1fn_x4
+ALU = mybir.AluOpType
+ACT = mybir.ActivationFunctionType
+
+P = 128
+PACK = 4
+PASS = P * PACK
+K_PASSES = K // PASS
+R_PASSES = H // PASS
+N_TILES = N // P
+BANK = 512
+
+
+def tile_list_cork_face_grading_kernel(
+    tc, tab_words, tab_scales, offs, pos1, pos2, w1, moist, gain, w4_words, w4_scales, out
+):
+    nc = tc.nc
+    with ExitStack() as ctx:
+        keep = ctx.enter_context(tc.tile_pool(name="keep", bufs=1))
+        ring = ctx.enter_context(tc.tile_pool(name="ring", bufs=2))
+        psum = ctx.enter_context(tc.psum_pool(name="psum", bufs=1))
+
+        def held(shape, dtype, name):
+            return keep.tile(shape, dtype, name=name, align_bytes=64)
+
+        def bank(i):
+            return psum.tile([P, BANK], F32, name="bank%d" % i)
+
+        offs_sb = keep.tile([P, S // 16], U16, name="offs_sb")
+        pos1_sb = keep.tile([P, M // 16], U16, name="pos1_sb")
+        pos2_sb = keep.tile([P, M // 16], U16, name="pos2_sb")
+        tabw = {}
+        tabs = held([P, T], U8, "slot_s")
+        vw = [held([P, S], U16, "vw%d" % a) for a in range(K_PASSES)]
+        vs = [held([P, S], U8, "vs%d" % a) for a in range(K_PASSES)]
+        HALF = PASS // 2
+        raw = {}
+        mo = {}
+        gain_sb = held([P, R_PASSES, PACK], F32, "gain_sb")
+        w4w = held([P, R_PASSES, 2 * N], U8, "w4w")
+        w4s = held([P, R_PASSES, N], U8, "w4s")
+        warm = held([P, 8], F32, "warm")
+
+        ROW0 = (0, 16, 48)
+        nc.vector.memset(tabs[64:128, :].bitcast(I32), 0)
+        nc.vector.memset(tabs[32:48, :].bitcast(I32), 0)
+        nc.gpsimd.memset(warm[:], 0.0)
+        for a in range(K_PASSES - 1):
+            nc.gpsimd.memset(vs[a][:].bitcast(I32), 0)
+        nc.gpsimd.memset(w4s[:].rearrange("p a n -> p (a n)").bitcast(I32), 0)
+        warm2 = held([P, 8], F32, "warm2")
+        nc.scalar.activation(warm2[:], warm[:], ACT.Tanh)
+
+        def load_w1(b, a, c0, c1, tag):
+            raw[b, a, c0] = held([P, PACK, c1 - c0], F32, tag)
+            cols = slice(b * PASS + c0, b * PASS + c1)
+            nc.sync.dma_start(
+                out=raw[b, a, c0][:],
+                in_=w1[a * PASS : (a + 1) * PASS, cols].rearrange("(p j) c -> p j c", j=PACK),
+            )
+
+        def load_tab(a, tag):
+            tabw[a] = held([P, T], U16, tag)
+            nc.sync.dma_start(out=tabw[a][:].bitcast(I32), in_=tab_words[a].bitcast(I32))
+
+        def load_moist(b, tag):
+            mo[b] = held([P, PACK, M], F32, tag)
+            rows = moist[b * PASS : (b + 1) * PASS, :].rearrange("(p t) m -> p t m", t=PACK)
+            for u in range(2):
+                nc.sync.dma_start(out=mo[b][:, 2 * u : 2 * u + 2, :], in_=rows[:, 2 * u : 2 * u + 2, :])
+
+        def load_w4s(q):
+            nc.gpsimd.dma_start(
+                out=w4s[32 * q : 32 * q + 4, :, :].bitcast(I32),
+                in_=w4_scales[:, 4 * q : 4 * q + 4, :].rearrange("a r n -> r a n").bitcast(I32),
+            )
+
+        nc.sync.dma_start(offs_sb[:], offs)
+        scale_rows = tab_scales.rearrange("a q t -> (a q) t").bitcast(I32)
+        nc.sync.dma_start(out=tabs[0:32, :].bitcast(I32), in_=scale_rows[0:32, :])
+        nc.sync.dma_start(out=tabs[48:64, :].bitcast(I32), in_=scale_rows[32:48, :])
+        load_tab(0, "slot_a")
+        nc.sync.dma_start(pos2_sb[:], pos2)
+        nc.sync.dma_start(pos1_sb[:], pos1)
+        load_tab(1, "slot_b")
+        load_w1(0, 0, 0, PASS, "slot_c")
+        nc.gpsimd.dma_start(out=gain_sb[:], in_=gain.rearrange("(b p t) -> p b t", p=P, t=PACK))
+        nc.gpsimd.dma_start(
+            out=w4w[:].bitcast(I32), in_=w4_words.rearrange("a p n -> p a n").bitcast(I32)
+        )
+        picked = held([P, S], U8, "picked")
+        nc.vector.tensor_copy(out=picked[:], in_=tabs[:].indirect(offs_sb[:]))
+
+        def place_scales(a):
+            for q in range(4):
+                row = ROW0[a] + 4 * q
+                nc.sync.dma_start(
+                    out=vs[a][32 * q : 32 * q + 4, :].bitcast(I32),
+                    in_=picked[row : row + 4, :].bitcast(I32),
+                )
+
+        place_scales(0)
+        load_tab(2, "slot_s")
+        place_scales(1)
+        for q in range(4):
+            load_w4s(q)
+        nc.gpsimd.memset(vs[2][:].bitcast(I32), 0)
+
+        wq = {}
+        ws = {}
+        grouped = {}
+
+        def cast_w1(b, a, c0, c1, on_vector):
+            if c0 == 0:
+                grouped[b, a] = ring.tile([P, PACK, P, PACK], BF16, name="grouped", align_bytes=64)
+            dst = grouped[b, a][:, :, c0 // PACK : c1 // PACK, :].rearrange("p t m j -> p m j t")
+            if (b, a, c0) in raw:
+                src = raw[b, a, c0][:, :, 0 : c1 - c0]
+            else:
+                src = raw[b, a, 0][:, :, c0:c1]
+            src = src.rearrange("p j (m t) -> p m j t", t=PACK)
+            if on_vector:
+                nc.vector.tensor_copy(out=dst, in_=src)
+            else:
+                nc.scalar.copy(out=dst, in_=src)
+
+        def pick_words(a):
+            nc.vector.tensor_copy(out=vw[a][:], in_=tabw[a][:].indirect(offs_sb[:]))
+
+        def quant_w1(b, a, t0=0, t1=PACK):
+            if t0 == 0:
+                wq[b, a] = held([P, PASS], U32, "wq%d%d" % (b, a))
+                ws[b, a] = held([P, PASS], U8, "ws%d%d" % (b, a))
+            nc.vector.quantize_mx(
+                out=wq[b, a][:, t0 * P : t1 * P].bitcast(FP8X4),
+                scales=ws[b, a][:, t0 * P : t1 * P],
+                in_=grouped[b, a][:, t0:t1, :, :].rearrange("p t m j -> p (t m j)"),
+            )
+
+        hb = {}
+
+        def first_pass(b, a, tiles=range(PACK)):
+            for t in tiles:
+                for v in range(2):
+                    if a == 0:
+                        hb[b, t, v] = bank(2 * t + v)
+                    nc.tensor.matmul_mx(
+                        out=hb[b, t, v][:],
+                        lhsT=wq[b, a][:, t * P : (t + 1) * P].bitcast(FP8X4),
+                        lhsT_scale=ws[b, a][:, t * P : (t + 1) * P],
+                        rhs=vw[a][:, v * BANK : (v + 1) * BANK].bitcast(FP4X4),
+                        rhs_scale=vs[a][:, v * BANK : (v + 1) * BANK],
+                        start=(a == 0),
+                        stop=(a == K_PASSES - 1),
+                    )
+
+        h = {}
+
+        def evac(b, t, split):
+            h[b, t] = held([P, S], F32, "h%d%d" % (b, t))
+            nc.scalar.copy(out=h[b, t][:, 0:BANK], in_=hb[b, t, 0][:])
+            if split:
+                nc.vector.tensor_copy(out=h[b, t][:, BANK:S], in_=hb[b, t, 1][:])
+            else:
+                nc.scalar.copy(out=h[b, t][:, BANK:S], in_=hb[b, t, 1][:])
+
+        pick_words(0)
+        load_w1(0, 1, 0, PASS, "slot_a")
+        place_scales(2)
+        cast_w1(0, 0, 0, PASS, False)
+        load_w1(0, 2, 0, HALF, "slot_c")
+        pick_words(1)
+        load_w1(0, 2, HALF, PASS, "slot_b")
+        quant_w1(0, 0)
+        first_pass(0, 0)
+        pick_words(2)
+        load_moist(0, "slot_s")
+        cast_w1(0, 1, 0, HALF, False)
+        cast_w1(0, 1, HALF, PASS, True)
+        load_w1(1, 0, 0, PASS, "slot_a")
+        quant_w1(0, 1)
+        cast_w1(0, 2, 0, HALF, False)
+        load_w1(1, 1, 0, PASS, "slot_c")
+        cast_w1(0, 2, HALF, PASS, True)
+        load_w1(1, 2, 0, PASS, "slot_b")
+        quant_w1(0, 2, 0, 2)
+        quant_w1(0, 2, 2, PACK)
+        first_pass(0, 1, [0, 1])
+        first_pass(0, 2, [0])
+        first_pass(0, 1, [2])
+        first_pass(0, 2, [1])
+        first_pass(0, 1, [3])
+        first_pass(0, 2, [2, 3])
+
+        xq = {}
+        xs = {}
+
+        def quant_x(key, xb, m0, m1):
+            if key not in xq:
+                xq[key] = held([P, M], U32, "xq%d%d" % key)
+                xs[key] = held([P, M], U8, "xs%d%d" % key)
+            nc.vector.quantize_mx(
+                out=xq[key][:, m0:m1].bitcast(FP8X4),
+                scales=xs[key][:, m0:m1],
+                in_=xb[:].rearrange("p m t -> p (m t)"),
+            )
+
+        dif = {}
+        difb = {}
+
+        def outer_pick(b, t):
+            if t == 0:
+                dif[b] = held([P, PACK, M], F32, "dif%d" % b)
+            nc.vector.tensor_tensor(
+                dif[b][:, t, :], h[b, t][:].indirect(pos2_sb[:]), mo[b][:, t, :], ALU.subtract
+            )
+
+        def outer_scale(b, t):
+            if t == 0:
+                if b == 0:
+                    difb[b] = ring.tile([P, PACK, M], BF16, name="grouped", align_bytes=64)
+                else:
+                    difb[b] = held([P, PACK, M], BF16, "late")
+            nc.scalar.activation(difb[b][:, t, :], dif[b][:, t, :], ACT.Copy, scale=gain_sb[:, b, t : t + 1])
+
+        def outer_weave(b):
+            xb = ring.tile([P, M, PACK], BF16, name="xb", align_bytes=64)
+            nc.vector.tensor_copy(
+                out=xb[:].rearrange("p (c i) t -> p c t i", i=4),
+                in_=difb[b][:].rearrange("p t (c i) -> p c t i", i=4),
+            )
+            return xb
+
+        def outer_gain(b):
+            xb = ring.tile([P, M, PACK], BF16, name="xb", align_bytes=64)
+            nc.vector.tensor_tensor(
+                xb[:].rearrange("p (c i) t -> p c t i", i=4),
+                dif[b][:].rearrange("p t (c i) -> p c t i", i=4),
+                gain_sb[:, b, :].unsqueeze(1).unsqueeze(3).to_broadcast([P, M // 4, PACK, 4]),
+                ALU.mult,
+            )
+            return xb
+
+        def inner_pick(b, m0, m1, flat):
+            sm = flat[:, PACK * m0 : PACK * m1].rearrange("p (t m) -> p t m", t=PACK)
+            whole = m1 - m0 == M
+            for t in range(PACK):
+                lst = pos1_sb[:] if whole else pos1_sb[:, m0 // 16 : m1 // 16]
+                nc.vector.tensor_tensor(
+                    sm[:, t, :], h[b, t][:].indirect(lst), mo[b][:, t, m0:m1], ALU.add
+                )
+            return sm
+
+        def inner_tanh(sm, w):
+            th = ring.tile([P, w, PACK], F32, name="th")
+            nc.scalar.activation(
+                th[:].rearrange("p (c i) t -> p c t i", i=4),
+                sm.rearrange("p t (c i) -> p c t i", i=4),
+                ACT.Tanh,
+            )
+            return th
+
+        def inner_gain(b, th, w):
+            if b == 0:
+                xb = held([P, w, PACK], BF16, "late")
+            else:
+                xb = ring.tile([P, w, PACK], BF16, name="xb", align_bytes=64)
+            nc.vector.tensor_tensor(
+                xb[:], th[:], gain_sb[:, b : b + 1, :].to_broadcast([P, w, PACK]), ALU.mult
+            )
+            return xb
+
+        def second(acc, c, b, key, m0, m1, start, stop):
+            nc.tensor.matmul_mx(
+                out=acc,
+                lhsT=w4w[:, b, 2 * P * c : 2 * P * (c + 1)].bitcast(FP4X4),
+                lhsT_scale=w4s[:, b, P * c : P * (c + 1)],
+                rhs=xq[key][:, m0:m1].bitcast(FP8X4),
+                rhs_scale=xs[key][:, m0:m1],
+                start=start,
+                stop=stop,
+            )
+
+        for t in range(PACK):
+            evac(0, t, t == 0)
+            outer_pick(0, t)
+        for a in range(K_PASSES):
+            if a == K_PASSES - 1:
+                cast_w1(1, a, 0, HALF, False)
+                cast_w1(1, a, HALF, PASS, True)
+            else:
+                cast_w1(1, a, 0, PASS, False)
+            if a == 0:
+                load_moist(1, "slot_a")
+            quant_w1(1, a)
+            first_pass(1, a)
+        sm0 = inner_pick(0, 0, M, held([P, PACK * M], F32, "sm0"))
+        for t in range(PACK):
+            outer_scale(0, t)
+        xb = outer_weave(0)
+        for t in range(PACK):
+            evac(1, t, False)
+            outer_pick(1, t)
+            if t == 0:
+                quant_x((0, 0), xb, 0, M)
+        th0 = inner_tanh(sm0, M)
+        yo = [bank(c) for c in range(N_TILES)]
+        for c in range(N_TILES):
+            second(yo[c][:], c, 0, (0, 0), 0, M, True, False)
+        for t in range(PACK):
+            outer_scale(1, t)
+        warm3 = held([P, 8], F32, "warm3")
+        nc.scalar.activation(warm3[:, 0:1], dif[1][:, PACK - 1, 0:1], ACT.Ln, bias=1.0, scale=0.0)
+        xb = outer_weave(1)
+        chunks = [(0, 256), (256, 384), (384, 512)]
+        flat1 = held([P, PACK * M], F32, "dif1")
+        quant_x((1, 0), xb, 0, M)
+        for c in range(N_TILES):
+            second(yo[c][:], c, 1, (1, 0), 0, M, False, True)
+        xbi = inner_gain(0, th0, M)
+        sms = [inner_pick(1, chunks[0][0], chunks[0][1], flat1)]
+        quant_x((0, 1), xbi, 0, M)
+        sms.append(inner_pick(1, chunks[1][0], chunks[1][1], flat1))
+        mag = held([P, N_TILES, M], F32, "mag")
+        lg = held([P, N_TILES, M], F32, "lg")
+        damp = mag
+        for c in range(N_TILES):
+            nc.scalar.activation(mag[:, c, :], yo[c][:], ACT.Abs)
+        nc.scalar.activation(lg[:], mag[:], ACT.Ln, bias=1.0)
+        ths = [inner_tanh(sms[0], 256)]
+        nc.scalar.activation(damp[:], lg[:], ACT.Exp, scale=-1.0)
+        out_v = out.rearrange("(c p) m -> p c m", p=P)
+        for i, (m0, m1) in enumerate(chunks):
+            if i == 0:
+                xb = inner_gain(1, ths[0], m1 - m0)
+                sms.append(inner_pick(1, chunks[2][0], chunks[2][1], flat1))
+            else:
+                xb = inner_gain(1, inner_tanh(sms[i], m1 - m0), m1 - m0)
+            quant_x((1, 1), xb, m0, m1)
+            for q in range(m0 // P, m1 // P):
+                yi = bank(4 + q)
+                for c in range(N_TILES):
+                    for b in range(R_PASSES):
+                        second(yi[:, c * P : (c + 1) * P], c, b, (b, 1), q * P, (q + 1) * P, b == 0, b == R_PASSES - 1)
+                res = held([P, N_TILES, P], F32, "res%d" % q)
+                nc.vector.tensor_tensor(
+                    res[:],
+                    yi[:, 0 : N_TILES * P].rearrange("p (c m) -> p c m", c=N_TILES),
+                    damp[:, :, q * P : (q + 1) * P],
+                    ALU.mult,
+                )
+                nc.sync.dma_start(out=out_v[:, :, q * P : (q + 1) * P], in_=res[:])

@@ -51,7 +51,6 @@ def tile_list_cork_face_grading_kernel(
         raw = {}
         mo = {}
         gain_sb = held([P, R_PASSES, PACK], F32, "gain_sb")
-        w4w = held([P, R_PASSES, 2 * N], U8, "w4w")
         w4s = held([P, R_PASSES, N], U8, "w4s")
         warm = held([P, 8], F32, "warm")
 
@@ -99,9 +98,6 @@ def tile_list_cork_face_grading_kernel(
         load_tab(1, "slot_b")
         load_w1(0, 0, 0, PASS, "slot_c")
         nc.gpsimd.dma_start(out=gain_sb[:], in_=gain.rearrange("(b p t) -> p b t", p=P, t=PACK))
-        nc.gpsimd.dma_start(
-            out=w4w[:].bitcast(I32), in_=w4_words.rearrange("a p n -> p a n").bitcast(I32)
-        )
         picked = held([P, S], U8, "picked")
         nc.vector.tensor_copy(out=picked[:], in_=tabs[:].indirect(offs_sb[:]))
 
@@ -123,10 +119,14 @@ def tile_list_cork_face_grading_kernel(
         wq = {}
         ws = {}
         grouped = {}
+        mix = held([P, 2 * M * K_PASSES], F32, "mix")
 
         def cast_w1(b, a, c0, c1, on_vector):
-            if c0 == 0:
-                grouped[b, a] = ring.tile([P, PACK, P, PACK], BF16, name="grouped", align_bytes=64)
+            if c0 == 0 and b == 0:
+                grouped[b, a] = ring.tile([P, PACK, P, PACK], BF16, name="grouped", align_bytes=64)[:]
+            if c0 == 0 and b == 1:
+                words = mix[:, 2 * M * a : 2 * M * (a + 1)]
+                grouped[b, a] = words.bitcast(BF16).rearrange("p (t m j) -> p t m j", t=PACK, j=PACK)
             dst = grouped[b, a][:, :, c0 // PACK : c1 // PACK, :].rearrange("p t m j -> p m j t")
             if (b, a, c0) in raw:
                 src = raw[b, a, c0][:, :, 0 : c1 - c0]
@@ -186,7 +186,6 @@ def tile_list_cork_face_grading_kernel(
         pick_words(1)
         load_w1(0, 2, HALF, PASS, "slot_b")
         quant_w1(0, 0)
-        first_pass(0, 0)
         pick_words(2)
         load_moist(0, "slot_s")
         cast_w1(0, 1, 0, HALF, False)
@@ -199,12 +198,9 @@ def tile_list_cork_face_grading_kernel(
         load_w1(1, 2, 0, PASS, "slot_b")
         quant_w1(0, 2, 0, 2)
         quant_w1(0, 2, 2, PACK)
-        first_pass(0, 1, [0, 1])
-        first_pass(0, 2, [0])
-        first_pass(0, 1, [2])
-        first_pass(0, 2, [1])
-        first_pass(0, 1, [3])
-        first_pass(0, 2, [2, 3])
+        for t in range(PACK):
+            for a in range(K_PASSES):
+                first_pass(0, a, [t])
 
         xq = {}
         xs = {}
@@ -232,18 +228,21 @@ def tile_list_cork_face_grading_kernel(
         def outer_scale(b, t):
             if t == 0:
                 if b == 0:
-                    difb[b] = ring.tile([P, PACK, M], BF16, name="grouped", align_bytes=64)
+                    difb[b] = held([P, PACK, M], BF16, "slot_c")
                 else:
                     difb[b] = held([P, PACK, M], BF16, "late")
             nc.scalar.activation(difb[b][:, t, :], dif[b][:, t, :], ACT.Copy, scale=gain_sb[:, b, t : t + 1])
 
-        def outer_weave(b):
-            xb = ring.tile([P, M, PACK], BF16, name="xb", align_bytes=64)
+        def weave(src, xb):
             nc.vector.tensor_copy(
                 out=xb[:].rearrange("p (c i) t -> p c t i", i=4),
-                in_=difb[b][:].rearrange("p t (c i) -> p c t i", i=4),
+                in_=src[:].rearrange("p t (c i) -> p c t i", i=4),
             )
             return xb
+
+        def outer_weave(b):
+            xb = ring.tile([P, M, PACK], BF16, name="xb", align_bytes=64)
+            return weave(difb[b], xb)
 
         def outer_gain(b):
             xb = ring.tile([P, M, PACK], BF16, name="xb", align_bytes=64)
@@ -256,7 +255,10 @@ def tile_list_cork_face_grading_kernel(
             return xb
 
         def inner_pick(b, m0, m1, flat):
-            sm = flat[:, PACK * m0 : PACK * m1].rearrange("p (t m) -> p t m", t=PACK)
+            if b == 0:
+                sm = flat[:].rearrange("p (t m) -> p t m", t=PACK)[:, :, 0:M]
+            else:
+                sm = flat[:, PACK * m0 : PACK * m1].rearrange("p (t m) -> p t m", t=PACK)
             whole = m1 - m0 == M
             for t in range(PACK):
                 lst = pos1_sb[:] if whole else pos1_sb[:, m0 // 16 : m1 // 16]
@@ -266,7 +268,10 @@ def tile_list_cork_face_grading_kernel(
             return sm
 
         def inner_tanh(sm, w):
-            th = ring.tile([P, w, PACK], F32, name="th")
+            if w == M:
+                th = held([P, w, PACK], F32, "wq12")
+            else:
+                th = ring.tile([P, w, PACK], F32, name="th")
             nc.scalar.activation(
                 th[:].rearrange("p (c i) t -> p c t i", i=4),
                 sm.rearrange("p t (c i) -> p c t i", i=4),
@@ -280,7 +285,7 @@ def tile_list_cork_face_grading_kernel(
             else:
                 xb = ring.tile([P, w, PACK], BF16, name="xb", align_bytes=64)
             nc.vector.tensor_tensor(
-                xb[:], th[:], gain_sb[:, b : b + 1, :].to_broadcast([P, w, PACK]), ALU.mult
+                xb[:], th, gain_sb[:, b : b + 1, :].to_broadcast([P, w, PACK]), ALU.mult
             )
             return xb
 
@@ -307,8 +312,14 @@ def tile_list_cork_face_grading_kernel(
             if a == 0:
                 load_moist(1, "slot_a")
             quant_w1(1, a)
-            first_pass(1, a)
-        sm0 = inner_pick(0, 0, M, held([P, PACK * M], F32, "sm0"))
+        w4w = held([P, R_PASSES, 2 * N], U8, "slot_b")
+        nc.sync.dma_start(
+            out=w4w[:].bitcast(I32), in_=w4_words.rearrange("a p n -> p a n").bitcast(I32)
+        )
+        for t in range(PACK):
+            for a in range(K_PASSES):
+                first_pass(1, a, [t])
+        sm0 = inner_pick(0, 0, M, mix)
         for t in range(PACK):
             outer_scale(0, t)
         xb = outer_weave(0)
@@ -317,50 +328,77 @@ def tile_list_cork_face_grading_kernel(
             outer_pick(1, t)
             if t == 0:
                 quant_x((0, 0), xb, 0, M)
-        th0 = inner_tanh(sm0, M)
+        th0 = held([P, PACK, M], F32, "wq12")
+        nc.scalar.activation(th0[:], sm0, ACT.Tanh)
         yo = [bank(c) for c in range(N_TILES)]
         for c in range(N_TILES):
             second(yo[c][:], c, 0, (0, 0), 0, M, True, False)
-        for t in range(PACK):
+        thb = held([P, PACK, M], BF16, "thb")
+
+        def inner_scale(t):
+            nc.scalar.activation(thb[:, t, :], th0[:, t, :], ACT.Copy, scale=gain_sb[:, 0, t : t + 1])
+
+        for t in range(PACK - 1):
             outer_scale(1, t)
+        inner_scale(0)
+        outer_scale(1, PACK - 1)
+        for t in range(1, PACK):
+            inner_scale(t)
         warm3 = held([P, 8], F32, "warm3")
-        nc.scalar.activation(warm3[:, 0:1], dif[1][:, PACK - 1, 0:1], ACT.Ln, bias=1.0, scale=0.0)
+        nc.scalar.activation(warm3[:, 0:1], th0[:, PACK - 1, 0:1], ACT.Ln, bias=1.0, scale=0.0)
         xb = outer_weave(1)
         chunks = [(0, 256), (256, 384), (384, 512)]
         flat1 = held([P, PACK * M], F32, "dif1")
         quant_x((1, 0), xb, 0, M)
         for c in range(N_TILES):
             second(yo[c][:], c, 1, (1, 0), 0, M, False, True)
-        xbi = inner_gain(0, th0, M)
+        xbi = weave(thb, held([P, M, PACK], BF16, "late"))
         sms = [inner_pick(1, chunks[0][0], chunks[0][1], flat1)]
         quant_x((0, 1), xbi, 0, M)
+        yi = [bank(4 + q) for q in range(M // P)]
+
+        def inner_pass(b, q):
+            for c in range(N_TILES):
+                first = b == 0 and c == 0
+                last = b == R_PASSES - 1 and c == N_TILES - 1
+                second(yi[q][:, c * P : (c + 1) * P], c, b, (b, 1), q * P, (q + 1) * P, first, last)
+
+        for q in range(M // P):
+            inner_pass(0, q)
         sms.append(inner_pick(1, chunks[1][0], chunks[1][1], flat1))
+        sms.append(inner_pick(1, chunks[2][0], chunks[2][1], flat1))
         mag = held([P, N_TILES, M], F32, "mag")
         lg = held([P, N_TILES, M], F32, "lg")
-        damp = mag
+        damp = held([P, N_TILES, M], F32, "damp")
         for c in range(N_TILES):
             nc.scalar.activation(mag[:, c, :], yo[c][:], ACT.Abs)
         nc.scalar.activation(lg[:], mag[:], ACT.Ln, bias=1.0)
-        ths = [inner_tanh(sms[0], 256)]
-        nc.scalar.activation(damp[:], lg[:], ACT.Exp, scale=-1.0)
         out_v = out.rearrange("(c p) m -> p c m", p=P)
+        th1 = held([P, M, PACK], F32, "mag")
+
+        def finish(q):
+            res = held([P, N_TILES, P], F32, "res%d" % q)
+            nc.vector.tensor_tensor(
+                res[:],
+                yi[q][:, 0 : N_TILES * P].rearrange("p (c m) -> p c m", c=N_TILES),
+                damp[:, :, q * P : (q + 1) * P],
+                ALU.mult,
+            )
+            nc.sync.dma_start(out=out_v[:, :, q * P : (q + 1) * P], in_=res[:])
+
         for i, (m0, m1) in enumerate(chunks):
-            if i == 0:
-                xb = inner_gain(1, ths[0], m1 - m0)
-                sms.append(inner_pick(1, chunks[2][0], chunks[2][1], flat1))
-            else:
-                xb = inner_gain(1, inner_tanh(sms[i], m1 - m0), m1 - m0)
+            th = th1[:, m0:m1, :]
+            nc.scalar.activation(
+                th.rearrange("p (c i) t -> p c t i", i=4),
+                sms[i].rearrange("p t (c i) -> p c t i", i=4),
+                ACT.Tanh,
+            )
+            nc.scalar.activation(damp[:, :, m0:m1], lg[:, :, m0:m1], ACT.Exp, scale=-1.0)
+            xb = inner_gain(1, th, m1 - m0)
+            if i > 0:
+                for q in range(chunks[i - 1][0] // P, chunks[i - 1][1] // P):
+                    finish(q)
             quant_x((1, 1), xb, m0, m1)
             for q in range(m0 // P, m1 // P):
-                yi = bank(4 + q)
-                for c in range(N_TILES):
-                    for b in range(R_PASSES):
-                        second(yi[:, c * P : (c + 1) * P], c, b, (b, 1), q * P, (q + 1) * P, b == 0, b == R_PASSES - 1)
-                res = held([P, N_TILES, P], F32, "res%d" % q)
-                nc.vector.tensor_tensor(
-                    res[:],
-                    yi[:, 0 : N_TILES * P].rearrange("p (c m) -> p c m", c=N_TILES),
-                    damp[:, :, q * P : (q + 1) * P],
-                    ALU.mult,
-                )
-                nc.sync.dma_start(out=out_v[:, :, q * P : (q + 1) * P], in_=res[:])
+                inner_pass(1, q)
+        finish(M // P - 1)

@@ -128,10 +128,8 @@ def tile_list_cork_face_grading_kernel(
                 words = mix[:, 2 * M * a : 2 * M * (a + 1)]
                 grouped[b, a] = words.bitcast(BF16).rearrange("p (t m j) -> p t m j", t=PACK, j=PACK)
             dst = grouped[b, a][:, :, c0 // PACK : c1 // PACK, :].rearrange("p t m j -> p m j t")
-            if (b, a, c0) in raw:
-                src = raw[b, a, c0][:, :, 0 : c1 - c0]
-            else:
-                src = raw[b, a, 0][:, :, c0:c1]
+            base = HALF if c0 >= HALF and (b, a, HALF) in raw else 0
+            src = raw[b, a, base][:, :, c0 - base : c1 - base]
             src = src.rearrange("p j (m t) -> p m j t", t=PACK)
             if on_vector:
                 nc.vector.tensor_copy(out=dst, in_=src)
@@ -182,9 +180,9 @@ def tile_list_cork_face_grading_kernel(
         load_w1(0, 1, 0, PASS, "slot_a")
         place_scales(2)
         cast_w1(0, 0, 0, PASS, False)
-        load_w1(0, 2, 0, HALF, "slot_c")
         pick_words(1)
-        load_w1(0, 2, HALF, PASS, "slot_b")
+        load_w1(0, 2, 0, HALF, "slot_b")
+        load_w1(0, 2, HALF, PASS, "slot_c")
         quant_w1(0, 0)
         pick_words(2)
         load_moist(0, "slot_s")
@@ -193,10 +191,12 @@ def tile_list_cork_face_grading_kernel(
         load_w1(1, 0, 0, PASS, "slot_a")
         quant_w1(0, 1)
         cast_w1(0, 2, 0, HALF, False)
-        load_w1(1, 1, 0, PASS, "slot_c")
-        cast_w1(0, 2, HALF, PASS, True)
-        load_w1(1, 2, 0, PASS, "slot_b")
-        quant_w1(0, 2, 0, 2)
+        load_w1(1, 1, 0, PASS, "slot_b")
+        cast_w1(0, 2, HALF, 416, True)
+        cast_w1(0, 2, 416, PASS, False)
+        load_w1(1, 2, 0, PASS, "slot_c")
+        quant_w1(0, 2, 0, 1)
+        quant_w1(0, 2, 1, 2)
         quant_w1(0, 2, 2, PACK)
         for t in range(PACK):
             for a in range(K_PASSES):
@@ -228,7 +228,7 @@ def tile_list_cork_face_grading_kernel(
         def outer_scale(b, t):
             if t == 0:
                 if b == 0:
-                    difb[b] = held([P, PACK, M], BF16, "slot_c")
+                    difb[b] = held([P, PACK, M], BF16, "slot_b")
                 else:
                     difb[b] = held([P, PACK, M], BF16, "late")
             nc.scalar.activation(difb[b][:, t, :], dif[b][:, t, :], ACT.Copy, scale=gain_sb[:, b, t : t + 1])
@@ -312,7 +312,7 @@ def tile_list_cork_face_grading_kernel(
             if a == 0:
                 load_moist(1, "slot_a")
             quant_w1(1, a)
-        w4w = held([P, R_PASSES, 2 * N], U8, "slot_b")
+        w4w = held([P, R_PASSES, 2 * N], U8, "slot_c")
         nc.sync.dma_start(
             out=w4w[:].bitcast(I32), in_=w4_words.rearrange("a p n -> p a n").bitcast(I32)
         )
@@ -323,13 +323,15 @@ def tile_list_cork_face_grading_kernel(
         for t in range(PACK):
             outer_scale(0, t)
         xb = outer_weave(0)
+        th0 = held([P, PACK, M], F32, "th0")
+        nc.scalar.activation(th0[:, 0:2, :], sm0[:, 0:2, :], ACT.Tanh)
         for t in range(PACK):
             evac(1, t, False)
             outer_pick(1, t)
             if t == 0:
                 quant_x((0, 0), xb, 0, M)
-        th0 = held([P, PACK, M], F32, "wq12")
-        nc.scalar.activation(th0[:], sm0, ACT.Tanh)
+            if t < 2:
+                nc.scalar.activation(th0[:, t + 2, :], sm0[:, t + 2, :], ACT.Tanh)
         yo = [bank(c) for c in range(N_TILES)]
         for c in range(N_TILES):
             second(yo[c][:], c, 0, (0, 0), 0, M, True, False)
@@ -338,16 +340,14 @@ def tile_list_cork_face_grading_kernel(
         def inner_scale(t):
             nc.scalar.activation(thb[:, t, :], th0[:, t, :], ACT.Copy, scale=gain_sb[:, 0, t : t + 1])
 
-        for t in range(PACK - 1):
+        for t in range(PACK):
             outer_scale(1, t)
-        inner_scale(0)
-        outer_scale(1, PACK - 1)
-        for t in range(1, PACK):
+        for t in range(PACK):
             inner_scale(t)
         warm3 = held([P, 8], F32, "warm3")
-        nc.scalar.activation(warm3[:, 0:1], th0[:, PACK - 1, 0:1], ACT.Ln, bias=1.0, scale=0.0)
+        nc.scalar.activation(warm3[:, 0:1], thb[:, PACK - 1, 0:1], ACT.Ln, bias=1.0, scale=0.0)
         xb = outer_weave(1)
-        chunks = [(0, 256), (256, 384), (384, 512)]
+        chunks = [(0, 256), (256, 512)]
         flat1 = held([P, PACK * M], F32, "dif1")
         quant_x((1, 0), xb, 0, M)
         for c in range(N_TILES):
@@ -366,7 +366,6 @@ def tile_list_cork_face_grading_kernel(
         for q in range(M // P):
             inner_pass(0, q)
         sms.append(inner_pick(1, chunks[1][0], chunks[1][1], flat1))
-        sms.append(inner_pick(1, chunks[2][0], chunks[2][1], flat1))
         mag = held([P, N_TILES, M], F32, "mag")
         lg = held([P, N_TILES, M], F32, "lg")
         damp = held([P, N_TILES, M], F32, "damp")
@@ -387,18 +386,16 @@ def tile_list_cork_face_grading_kernel(
             nc.sync.dma_start(out=out_v[:, :, q * P : (q + 1) * P], in_=res[:])
 
         for i, (m0, m1) in enumerate(chunks):
-            th = th1[:, m0:m1, :]
             nc.scalar.activation(
-                th.rearrange("p (c i) t -> p c t i", i=4),
+                th1[:, m0:m1, :].rearrange("p (c i) t -> p c t i", i=4),
                 sms[i].rearrange("p t (c i) -> p c t i", i=4),
                 ACT.Tanh,
             )
-            nc.scalar.activation(damp[:, :, m0:m1], lg[:, :, m0:m1], ACT.Exp, scale=-1.0)
-            xb = inner_gain(1, th, m1 - m0)
-            if i > 0:
-                for q in range(chunks[i - 1][0] // P, chunks[i - 1][1] // P):
-                    finish(q)
+        nc.scalar.activation(damp[:], lg[:], ACT.Exp, scale=-1.0)
+        for m0, m1 in chunks:
+            xb = inner_gain(1, th1[:, m0:m1, :], m1 - m0)
             quant_x((1, 1), xb, m0, m1)
             for q in range(m0 // P, m1 // P):
                 inner_pass(1, q)
-        finish(M // P - 1)
+        for q in range(M // P):
+            finish(q)

from contextlib import ExitStack

import concourse.mybir as mybir

K, T, S, M, H, N = 1536, 4096, 1024, 512, 1024, 384
FLOPS = 2 * K * H * S + 2 * H * N * 2 * M

F32 = mybir.dt.float32
BF16 = mybir.dt.bfloat16
I32 = mybir.dt.int32
U32 = mybir.dt.uint32
U16 = mybir.dt.uint16
U8 = mybir.dt.uint8
FP8X4 = mybir.dt.float8_e4m3fn_x4
FP4X4 = mybir.dt.float4_e2m1fn_x4
ALU = mybir.AluOpType
ACT = mybir.ActivationFunctionType

P = 128
PACK = 4
PASS = P * PACK
K_PASSES = K // PASS
R_PASSES = H // PASS
N_TILES = N // P
BANK = 512


def tile_list_cork_face_grading_kernel(
    tc, tab_words, tab_scales, offs, pos1, pos2, w1, moist, gain, w4_words, w4_scales, out
):
    nc = tc.nc
    with ExitStack() as ctx:
        keep = ctx.enter_context(tc.tile_pool(name="keep", bufs=1))
        ring = ctx.enter_context(tc.tile_pool(name="ring", bufs=2))
        psum = ctx.enter_context(tc.psum_pool(name="psum", bufs=1))

        def held(shape, dtype, name):
            return keep.tile(shape, dtype, name=name, align_bytes=64)

        def bank(i):
            return psum.tile([P, BANK], F32, name="bank%d" % i)

        offs_sb = keep.tile([P, S // 16], U16, name="offs_sb")
        pos1_sb = keep.tile([P, M // 16], U16, name="pos1_sb")
        pos2_sb = keep.tile([P, M // 16], U16, name="pos2_sb")
        tabw = {}
        tabs = held([P, T], U8, "slot_s")
        vw = [held([P, S], U16, "vw%d" % a) for a in range(K_PASSES)]
        vs = [held([P, S], U8, "vs%d" % a) for a in range(K_PASSES)]
        HALF = PASS // 2
        raw = {}
        mo = {}
        gain_sb = held([P, R_PASSES, PACK], F32, "gain_sb")
        w4s = held([P, R_PASSES, N], U8, "w4s")
        warm = held([P, 8], F32, "warm")

        ROW0 = (0, 16, 48)
        nc.vector.memset(tabs[64:128, :].bitcast(I32), 0)
        nc.vector.memset(tabs[32:48, :].bitcast(I32), 0)
        nc.gpsimd.memset(warm[:], 0.0)
        for a in range(K_PASSES - 1):
            nc.gpsimd.memset(vs[a][:].bitcast(I32), 0)
        nc.gpsimd.memset(w4s[:].rearrange("p a n -> p (a n)").bitcast(I32), 0)
        warm2 = held([P, 8], F32, "warm2")
        nc.scalar.activation(warm2[:], warm[:], ACT.Tanh)

        def load_w1(b, a, c0, c1, tag):
            raw[b, a, c0] = held([P, PACK, c1 - c0], F32, tag)
            cols = slice(b * PASS + c0, b * PASS + c1)
            nc.sync.dma_start(
                out=raw[b, a, c0][:],
                in_=w1[a * PASS : (a + 1) * PASS, cols].rearrange("(p j) c -> p j c", j=PACK),
            )

        def load_tab(a, tag):
            tabw[a] = held([P, T], U16, tag)
            nc.sync.dma_start(out=tabw[a][:].bitcast(I32), in_=tab_words[a].bitcast(I32))

        def load_moist(b, tag):
            mo[b] = held([P, PACK, M], F32, tag)
            rows = moist[b * PASS : (b + 1) * PASS, :].rearrange("(p t) m -> p t m", t=PACK)
            for u in range(2):
                nc.sync.dma_start(out=mo[b][:, 2 * u : 2 * u + 2, :], in_=rows[:, 2 * u : 2 * u + 2, :])

        def load_w4s(q):
            nc.gpsimd.dma_start(
                out=w4s[32 * q : 32 * q + 4, :, :].bitcast(I32),
                in_=w4_scales[:, 4 * q : 4 * q + 4, :].rearrange("a r n -> r a n").bitcast(I32),
            )

        nc.sync.dma_start(offs_sb[:], offs)
        scale_rows = tab_scales.rearrange("a q t -> (a q) t").bitcast(I32)
        nc.sync.dma_start(out=tabs[0:32, :].bitcast(I32), in_=scale_rows[0:32, :])
        nc.sync.dma_start(out=tabs[48:64, :].bitcast(I32), in_=scale_rows[32:48, :])
        load_tab(0, "slot_a")
        nc.sync.dma_start(pos2_sb[:], pos2)
        nc.sync.dma_start(pos1_sb[:], pos1)
        load_tab(1, "slot_b")
        load_w1(0, 0, 0, PASS, "slot_c")
        nc.gpsimd.dma_start(out=gain_sb[:], in_=gain.rearrange("(b p t) -> p b t", p=P, t=PACK))
        picked = held([P, S], U8, "picked")
        nc.vector.tensor_copy(out=picked[:], in_=tabs[:].indirect(offs_sb[:]))

        def place_scales(a):
            for q in range(4):
                row = ROW0[a] + 4 * q
                nc.sync.dma_start(
                    out=vs[a][32 * q : 32 * q + 4, :].bitcast(I32),
                    in_=picked[row : row + 4, :].bitcast(I32),
                )

        place_scales(0)
        load_tab(2, "slot_s")
        place_scales(1)
        for q in range(4):
            load_w4s(q)
        nc.gpsimd.memset(vs[2][:].bitcast(I32), 0)

        wq = {}
        ws = {}
        grouped = {}
        mix = held([P, 2 * M * K_PASSES], F32, "mix")

        def cast_w1(b, a, c0, c1, on_vector):
            if c0 == 0 and b == 0:
                grouped[b, a] = ring.tile([P, PACK, P, PACK], BF16, name="grouped", align_bytes=64)[:]
            if c0 == 0 and b == 1:
                words = mix[:, 2 * M * a : 2 * M * (a + 1)]
                grouped[b, a] = words.bitcast(BF16).rearrange("p (t m j) -> p t m j", t=PACK, j=PACK)
            dst = grouped[b, a][:, :, c0 // PACK : c1 // PACK, :].rearrange("p t m j -> p m j t")
            base = HALF if c0 >= HALF and (b, a, HALF) in raw else 0
            src = raw[b, a, base][:, :, c0 - base : c1 - base]
            src = src.rearrange("p j (m t) -> p m j t", t=PACK)
            if on_vector:
                nc.vector.tensor_copy(out=dst, in_=src)
            else:
                nc.scalar.copy(out=dst, in_=src)

        def pick_words(a):
            nc.vector.tensor_copy(out=vw[a][:], in_=tabw[a][:].indirect(offs_sb[:]))

        def quant_w1(b, a, t0=0, t1=PACK):
            if t0 == 0:
                wq[b, a] = held([P, PASS], U32, "wq%d%d" % (b, a))
                ws[b, a] = held([P, PASS], U8, "ws%d%d" % (b, a))
            nc.vector.quantize_mx(
                out=wq[b, a][:, t0 * P : t1 * P].bitcast(FP8X4),
                scales=ws[b, a][:, t0 * P : t1 * P],
                in_=grouped[b, a][:, t0:t1, :, :].rearrange("p t m j -> p (t m j)"),
            )

        hb = {}

        def first_pass(b, a, tiles=range(PACK)):
            for t in tiles:
                for v in range(2):
                    if a == 0:
                        hb[b, t, v] = bank(2 * t + v)
                    nc.tensor.matmul_mx(
                        out=hb[b, t, v][:],
                        lhsT=wq[b, a][:, t * P : (t + 1) * P].bitcast(FP8X4),
                        lhsT_scale=ws[b, a][:, t * P : (t + 1) * P],
                        rhs=vw[a][:, v * BANK : (v + 1) * BANK].bitcast(FP4X4),
                        rhs_scale=vs[a][:, v * BANK : (v + 1) * BANK],
                        start=(a == 0),
                        stop=(a == K_PASSES - 1),
                    )

        h = {}

        def evac(b, t, split):
            h[b, t] = held([P, S], F32, "h%d%d" % (b, t))
            nc.scalar.copy(out=h[b, t][:, 0:BANK], in_=hb[b, t, 0][:])
            if split:
                nc.vector.tensor_copy(out=h[b, t][:, BANK:S], in_=hb[b, t, 1][:])
            else:
                nc.scalar.copy(out=h[b, t][:, BANK:S], in_=hb[b, t, 1][:])

        pick_words(0)
        load_w1(0, 1, 0, PASS, "slot_a")
        place_scales(2)
        cast_w1(0, 0, 0, PASS, False)
        pick_words(1)
        load_w1(0, 2, 0, HALF, "slot_b")
        load_w1(0, 2, HALF, PASS, "slot_c")
        quant_w1(0, 0)
        pick_words(2)
        load_moist(0, "slot_s")
        cast_w1(0, 1, 0, HALF, False)
        cast_w1(0, 1, HALF, PASS, True)
        load_w1(1, 0, 0, PASS, "slot_a")
        quant_w1(0, 1)
        cast_w1(0, 2, 0, HALF, False)
        load_w1(1, 1, 0, PASS, "slot_b")
        cast_w1(0, 2, HALF, 416, True)
        cast_w1(0, 2, 416, PASS, False)
        load_w1(1, 2, 0, PASS, "slot_c")
        quant_w1(0, 2, 0, 1)
        quant_w1(0, 2, 1, 2)
        quant_w1(0, 2, 2, PACK)
        for t in range(PACK):
            for a in range(K_PASSES):
                first_pass(0, a, [t])

        xq = {}
        xs = {}

        def quant_x(key, xb, m0, m1):
            if key not in xq:
                xq[key] = held([P, M], U32, "xq%d%d" % key)
                xs[key] = held([P, M], U8, "xs%d%d" % key)
            nc.vector.quantize_mx(
                out=xq[key][:, m0:m1].bitcast(FP8X4),
                scales=xs[key][:, m0:m1],
                in_=xb[:].rearrange("p m t -> p (m t)"),
            )

        dif = {}
        difb = {}

        def outer_pick(b, t):
            if t == 0:
                dif[b] = held([P, PACK, M], F32, "dif%d" % b)
            nc.vector.tensor_tensor(
                dif[b][:, t, :], h[b, t][:].indirect(pos2_sb[:]), mo[b][:, t, :], ALU.subtract
            )

        def outer_scale(b, t):
            if t == 0:
                if b == 0:
                    difb[b] = held([P, PACK, M], BF16, "slot_b")
                else:
                    difb[b] = held([P, PACK, M], BF16, "late")
            nc.scalar.activation(difb[b][:, t, :], dif[b][:, t, :], ACT.Copy, scale=gain_sb[:, b, t : t + 1])

        def weave(src, xb):
            nc.vector.tensor_copy(
                out=xb[:].rearrange("p (c i) t -> p c t i", i=4),
                in_=src[:].rearrange("p t (c i) -> p c t i", i=4),
            )
            return xb

        def outer_weave(b):
            xb = ring.tile([P, M, PACK], BF16, name="xb", align_bytes=64)
            return weave(difb[b], xb)

        def outer_gain(b):
            xb = ring.tile([P, M, PACK], BF16, name="xb", align_bytes=64)
            nc.vector.tensor_tensor(
                xb[:].rearrange("p (c i) t -> p c t i", i=4),
                dif[b][:].rearrange("p t (c i) -> p c t i", i=4),
                gain_sb[:, b, :].unsqueeze(1).unsqueeze(3).to_broadcast([P, M // 4, PACK, 4]),
                ALU.mult,
            )
            return xb

        def inner_pick(b, m0, m1, flat):
            if b == 0:
                sm = flat[:].rearrange("p (t m) -> p t m", t=PACK)[:, :, 0:M]
            else:
                sm = flat[:, PACK * m0 : PACK * m1].rearrange("p (t m) -> p t m", t=PACK)
            whole = m1 - m0 == M
            for t in range(PACK):
                lst = pos1_sb[:] if whole else pos1_sb[:, m0 // 16 : m1 // 16]
                nc.vector.tensor_tensor(
                    sm[:, t, :], h[b, t][:].indirect(lst), mo[b][:, t, m0:m1], ALU.add
                )
            return sm

        def inner_tanh(sm, w):
            if w == M:
                th = held([P, w, PACK], F32, "wq12")
            else:
                th = ring.tile([P, w, PACK], F32, name="th")
            nc.scalar.activation(
                th[:].rearrange("p (c i) t -> p c t i", i=4),
                sm.rearrange("p t (c i) -> p c t i", i=4),
                ACT.Tanh,
            )
            return th

        def inner_gain(b, th, w):
            if b == 0:
                xb = held([P, w, PACK], BF16, "late")
            else:
                xb = ring.tile([P, w, PACK], BF16, name="xb", align_bytes=64)
            nc.vector.tensor_tensor(
                xb[:], th, gain_sb[:, b : b + 1, :].to_broadcast([P, w, PACK]), ALU.mult
            )
            return xb

        def second(acc, c, b, key, m0, m1, start, stop):
            nc.tensor.matmul_mx(
                out=acc,
                lhsT=w4w[:, b, 2 * P * c : 2 * P * (c + 1)].bitcast(FP4X4),
                lhsT_scale=w4s[:, b, P * c : P * (c + 1)],
                rhs=xq[key][:, m0:m1].bitcast(FP8X4),
                rhs_scale=xs[key][:, m0:m1],
                start=start,
                stop=stop,
            )

        for t in range(PACK):
            evac(0, t, t == 0)
            outer_pick(0, t)
        for a in range(K_PASSES):
            if a == K_PASSES - 1:
                cast_w1(1, a, 0, HALF, False)
                cast_w1(1, a, HALF, PASS, True)
            else:
                cast_w1(1, a, 0, PASS, False)
            if a == 0:
                load_moist(1, "slot_a")
            quant_w1(1, a)
        w4w = held([P, R_PASSES, 2 * N], U8, "slot_c")
        nc.sync.dma_start(
            out=w4w[:].bitcast(I32), in_=w4_words.rearrange("a p n -> p a n").bitcast(I32)
        )
        for t in range(PACK):
            for a in range(K_PASSES):
                first_pass(1, a, [t])
        sm0 = inner_pick(0, 0, M, mix)
        for t in range(PACK):
            outer_scale(0, t)
        xb = outer_weave(0)
        th0 = held([P, PACK, M], F32, "th0")
        nc.scalar.activation(th0[:, 0:2, :], sm0[:, 0:2, :], ACT.Tanh)
        for t in range(PACK):
            evac(1, t, False)
            outer_pick(1, t)
            if t == 0:
                quant_x((0, 0), xb, 0, M)
            if t < 2:
                nc.scalar.activation(th0[:, t + 2, :], sm0[:, t + 2, :], ACT.Tanh)
        yo = [bank(c) for c in range(N_TILES)]
        for c in range(N_TILES):
            second(yo[c][:], c, 0, (0, 0), 0, M, True, False)
        thb = held([P, PACK, M], BF16, "thb")

        def inner_scale(t):
            nc.scalar.activation(thb[:, t, :], th0[:, t, :], ACT.Copy, scale=gain_sb[:, 0, t : t + 1])

        for t in range(PACK):
            outer_scale(1, t)
        for t in range(PACK):
            inner_scale(t)
        warm3 = held([P, 8], F32, "warm3")
        nc.scalar.activation(warm3[:, 0:1], thb[:, PACK - 1, 0:1], ACT.Ln, bias=1.0, scale=0.0)
        xb = outer_weave(1)
        chunks = [(0, 256), (256, 512)]
        flat1 = held([P, PACK * M], F32, "dif1")
        quant_x((1, 0), xb, 0, M)
        for c in range(N_TILES):
            second(yo[c][:], c, 1, (1, 0), 0, M, False, True)
        xbi = weave(thb, held([P, M, PACK], BF16, "late"))
        sms = [inner_pick(1, chunks[0][0], chunks[0][1], flat1)]
        quant_x((0, 1), xbi, 0, M)
        yi = [bank(4 + q) for q in range(M // P)]

        def inner_pass(b, q):
            for c in range(N_TILES):
                first = b == 0 and c == 0
                last = b == R_PASSES - 1 and c == N_TILES - 1
                second(yi[q][:, c * P : (c + 1) * P], c, b, (b, 1), q * P, (q + 1) * P, first, last)

        for q in range(M // P):
            inner_pass(0, q)
        sms.append(inner_pick(1, chunks[1][0], chunks[1][1], flat1))
        mag = held([P, N_TILES, M], F32, "mag")
        lg = held([P, N_TILES, M], F32, "lg")
        damp = held([P, N_TILES, M], F32, "damp")
        for c in range(N_TILES):
            nc.scalar.activation(mag[:, c, :], yo[c][:], ACT.Abs)
        nc.scalar.activation(lg[:], mag[:], ACT.Ln, bias=1.0)
        out_v = out.rearrange("(c p) m -> p c m", p=P)
        th1 = held([P, M, PACK], F32, "mag")

        def finish(q):
            res = held([P, N_TILES, P], F32, "res%d" % q)
            nc.vector.tensor_tensor(
                res[:],
                yi[q][:, 0 : N_TILES * P].rearrange("p (c m) -> p c m", c=N_TILES),
                damp[:, :, q * P : (q + 1) * P],
                ALU.mult,
            )
            nc.sync.dma_start(out=out_v[:, :, q * P : (q + 1) * P], in_=res[:])

        for i, (m0, m1) in enumerate(chunks):
            nc.scalar.activation(
                th1[:, m0:m1, :].rearrange("p (c i) t -> p c t i", i=4),
                sms[i].rearrange("p t (c i) -> p c t i", i=4),
                ACT.Tanh,
            )
        nc.scalar.activation(damp[:], lg[:], ACT.Exp, scale=-1.0)
        for m0, m1 in chunks:
            xb = inner_gain(1, th1[:, m0:m1, :], m1 - m0)
            quant_x((1, 1), xb, m0, m1)
            for q in range(m0 // P, m1 // P):
                inner_pass(1, q)
        for q in range(M // P):
            finish(q)
